import numpy as np, ml_dtypes
CORES = [16,18,20,22]
N = 4
BF = ml_dtypes.bfloat16
LA, SUB, W, V, VIS, TRY, R1, R2 = 256, 16, 4096, 4096, 5, 2, 9, 12
A = [5, 4, 3, 3, 2]
def levels(rng, n, lo, hi):
    return np.minimum((np.exp2(lo + (hi - lo) * rng.random((N, 8, 1, n))) * rng.random((N, 8, 16, n))).astype(np.int64), 255)
def slots(rng):
    share = rng.choice(np.array([0.3, 0.6, 0.9, 1.0]), (N, 8, 1, LA))
    return np.where(rng.random((N, 8, 16, LA)) < share, rng.integers(0, W, (N, 8, 16, LA)), -1)
def parts(rng):
    return (levels(rng, W, 6.5, 9.0), levels(rng, V, 5.5, 9.0), slots(rng), levels(rng, LA, 6.5, 9.0), rng.integers(1, 256, (N, 8, 16)), rng.integers(0, 256, (N, 8, 16)))
def pack(x, c, s, z, w, p):
    b = lambda v: np.ascontiguousarray(v.reshape(N, 128, -1)).astype(np.float32).astype(BF)
    i = lambda v: np.ascontiguousarray(v.reshape(N, 128, -1)).astype(np.int32)
    return {"x0": b(x), "cl": b(c), "sl": i(s), "z0": b(z), "wt": i(w), "kp": i(p)}
def setup_inputs(rng):
    return pack(*parts(rng))
def setup_inputs_spread(rng):
    x, c, s, z, w, p = parts(rng)
    x, c, z = levels(rng, W, 0.0, 9.0), levels(rng, V, 0.0, 9.0), levels(rng, LA, 0.0, 9.0)
    w = np.clip(np.exp2(8 * rng.random(w.shape)).astype(np.int64), 1, 255); p = np.clip(np.exp2(8 * rng.random(p.shape)).astype(np.int64) - 1, 0, 255)
    return pack(x, c, s, z, w, p)
def setup_inputs_ends(rng):
    e = lambda n, d: 255 * (rng.random((N, 8, 16, n)) < rng.choice(np.array(d), (N, 8, 1, n))).astype(np.int64)
    x, c, z = e(W, [0.3, 0.6, 0.9]), e(V, [0.0, 0.5, 0.9, 1.0]), e(LA, [0.3, 0.6, 0.9])
    r = rng.random((N, 8, 16, LA))
    s = np.where(r < 0.35, -1, np.where(r < 0.7, W - 1, np.where(r < 0.8, 0, rng.integers(0, W, r.shape))))
    w = np.where(rng.random((N, 8, 16)) < 0.5, 1, 255); w[:, :, 13:15] = 1; w[:, :, 15] = 255; w[:, 6] = 255
    p = 255 * rng.integers(0, 2, (N, 8, 16)); p[:, 7, 0] = 255; p[:, 7, 15] = 255; p[:, 7, 1] = 0
    x[..., W - 1] = 255
    for i in (0, LA - 1):
        z[..., i] = 0; z[:, :, 13:, i] = 255; s[:, :, 0, i] = W - 1
    for i in (1, LA - 2): z[..., i] = 255
    for i in (2, LA - 3): z[..., i] = 0
    return pack(x, c, s, z, w, p)
def setup_inputs_corners(rng):
    x, c, s, z, w, p = parts(rng); x[..., 0] = 255; x[..., W - 1] = 0
    kind = rng.integers(0, 10, (N, 8, 1, LA)); kind[..., :10] = np.arange(10); kind[..., LA - 10:] = np.arange(10)
    k = np.arange(16)[:, None]; o = np.argsort(rng.random((N, 8, 16, LA)), axis=2); any_ = rng.integers(0, W, s.shape)
    low = np.arange(LA) < LA // 2
    s = np.where(kind == 0, -1, s); s = np.where(kind == 1, any_, s)
    s = np.where(kind == 2, np.where(k == np.where(low, 13, 15), 0, W - 1), s)
    s = np.where(kind == 3, np.where(o < TRY, 0, W - 1), s); s = np.where(kind == 4, np.where(o < TRY + 1, 0, W - 1), s)
    s = np.where(kind == 5, np.where(k == 15, any_, -1), s); s = np.where(kind == 6, np.where(k == 15, -1, any_), s)
    s = np.where(kind == 7, SUB * np.arange(LA) + any_ % SUB, s); s = np.where(kind == 8, any_[:, :, :1], s)
    z = np.where(kind == 1, 255, z); z = np.where((kind >= 2) & (kind <= 4), np.minimum(z, 254), z); z = np.where((kind == 2) & low, 254, z)
    for q in range(N):
        g = rng.permutation(8)
        c[q, g[:2]] = 0; c[q, g[2:4]] = 255
        w[q, g[0]] = 1; w[q, g[2]] = 255; w[q, g[4]] = 255; w[q, g[5]] = 1; p[q, g[3]] = 0; p[q, g[5]] = 255; p[q, g[6]] = 0
    return pack(x, c, s, z, w, p)
def setup_inputs_ties(rng):
    x, c, s, z, w, p = parts(rng)
    x, c, z = 85 * (x >> 6), 85 * (c >> 6), 85 * (z >> 6)
    x[..., 1::2] = x[..., ::2]
    same = np.take_along_axis(x, np.maximum(s[:, :, 3:4], 0), 3)
    z = np.where(rng.random((N, 8, 1, LA)) < 0.5, same, z)
    return pack(x, c, s, z, w, p)
def setup_inputs_bits(rng):
    x, c, s, z, w, p = parts(rng); k = np.arange(16)[:, None]
    one = k == rng.integers(0, 16, (N, 8, 1, 1))
    x[..., 0] = 255; x[..., W - 2] = 0; x[..., W - 1:] = np.where(one, 255, 0)
    kind = rng.choice(np.array([0, 0, 1, 2, 3, 3]), (N, 1, 1, LA))
    m = np.where(kind == 0, 8, 1 + 2 * rng.integers(0, 4, kind.shape)); on = np.argsort(rng.random((N, 8, 1, LA)), axis=1) < m
    first = np.where(kind == 1, 0, TRY - 1)
    v = np.where(k < first, W - 1, np.where(k == first, 0, s))
    v = np.where(on, v, np.where(rng.random((N, 8, 1, LA)) < 0.5, -1, W - 2))
    s = np.where(kind < 3, v, s)
    high = 255 - (rng.random((N, 8, 16, LA)) < rng.choice(np.array([0.0, 0.5, 1.0]), (N, 1, 1, LA))).astype(np.int64)
    z = np.where(kind < 3, np.where(one, 254, high), z)
    w[:, 7] = 255
    return pack(x, c, s, z, w, p)
def check_inputs(d):
    bad = []
    for k, lo, hi in (("x0", 0, 255), ("cl", 0, 255), ("sl", -1, W - 1), ("z0", 0, 255), ("wt", 1, 255), ("kp", 0, 255)):
        v = np.asarray(d[k]).astype(np.float32)
        if np.min(v) < lo or np.max(v) > hi or np.any(v != np.floor(v)): bad.append("range of " + k)
    return bad
def hashes(v, w, p, t):
    u = np.add.reduce(w * v, axis=2) & (V - 1)
    return u, ((u * u >> 5)[:, :, None] + p * u[:, :, None] + 97 * t) & (V - 1)
def reference(x0, cl, sl, z0, wt, kp):
    x = x0.astype(np.float32).astype(np.int32).reshape(N, 8, 16, W); c = cl.astype(np.float32).astype(np.int32).reshape(N, 8, 16, V)
    z = z0.astype(np.float32).astype(np.int32).reshape(N, 8, 16, LA); s = sl.astype(np.int32).reshape(N, 8, 16, LA)
    w = wt.astype(np.int32).reshape(N, 8, 16, 1); p = kp.astype(np.int32).reshape(N, 8, 16, 1)
    bit = np.zeros((N, LA), np.int64); k16 = np.arange(16)[:, None]
    for t in range(VIS):
        J = (np.arange(N) + 1 + t % (N - 1)) % N
        filled = s >= 0
        old = np.take_along_axis(x, np.maximum(s, 0).reshape(N, 8, 1, 16 * LA), 3).reshape(N, 8, 16, 16, LA)
        m = np.minimum(z[:, :, :, None], old)
        free = filled & (np.add.reduce(m, axis=2) < np.add.reduce(old, axis=2))
        done = np.zeros((N, 8, LA), bool); best = z; put = np.zeros((N, 8, LA), np.int64)
        for trial in range(TRY):
            has = np.any(free, axis=2) & ~done; k = np.argmax(free, axis=2)
            cand = np.take_along_axis(m, k[:, :, None, None], 3)[:, :, :, 0]
            h = hashes(cand, w[J], p[J], t)[1]
            b = np.take_along_axis(c[J], h.reshape(N, 8, 1, 16 * LA), 3).reshape(N, 8, 16, 16, LA)
            met = np.add.reduce((b <= cand[:, :, :, None]).astype(np.int32), axis=2) >= R1
            neg = has & (np.add.reduce(met.astype(np.int32), axis=2) >= A[t] + bit[J][:, None])
            bit[J] = np.add.reduce(neg.astype(np.int64), axis=1) & 1
            best = np.where(neg[:, :, None], cand, best); put = np.where(neg, k, put); done = done | neg
            free = free & (k16 != k[:, :, None])
        put = np.where(done, put, np.where(np.any(~filled, axis=2), np.argmax(~filled, axis=2), t))
        n = SUB * np.arange(LA) + (hashes(best, w, p, t)[0] & (SUB - 1))
        near = filled & (np.add.reduce((old <= best[:, :, :, None]).astype(np.int32), axis=2) >= R2)
        v = np.maximum(best, np.maximum.reduce(np.where(near[:, :, None], old, 0), axis=3))
        h0 = hashes(v, w, p, t)[1][:, :, :1]
        z = np.abs(v - np.take_along_axis(c, h0, 3))
        np.put_along_axis(x, np.ascontiguousarray(np.broadcast_to(n[:, :, None], (N, 8, 16, LA))), best, 3)
        s = np.where(k16 == put[:, :, None], n[:, :, None], s)
    return {"yx": x.reshape(N, 128, W).astype(np.float32).astype(BF), "yl": s.reshape(N, 128, LA).astype(np.float32), "yz": z.reshape(N, 128, LA).astype(np.float32).astype(BF)}

import numpy as np
from concourse.mybir import dt, AluOpType as A, ActivationFunctionType as F

N, VIS = 4, 5
AT = [5, 4, 3, 3, 2]
H = 2
L = 256 // H
NB = L // 16
PAD = 16
SK_A = 8
SK_D = 8
SM_B = 5
GV = 1
BON = {"A0": 28000, "B0": 16000, "C0": 6000, "D0": 10000, "O1": -12000, "D1": 5000, "O0": 81000, "C1": 7000, "A1": 7000, "B1": 14000}
NP = 4
TC = 0.417
VCY, GCY, LAT = 0.83, 1.56, 120.0

SCRATCH = {}
SEMAPHORES = ["eV", "eS", "eT", "eG", "ls", "out"]


def _sb(name, cols, dtype):
    SCRATCH[name] = ("sbuf", [128, cols], dtype)


for _b in range(8):
    SCRATCH["p%d" % _b] = ("psum", [128, 512], "float32")
_sb("X", 4096 + PAD, "bfloat16")
for _d in range(4):
    _sb("C%d" % _d, 4096, "bfloat16")
    _sb("WA%d" % _d, 2048, "bfloat16")
    _sb("WK%d" % _d, 2, "float32")
    if _d:
        _sb("KD%d" % _d, 2048, "float16")
    _sb("KR%d" % _d, 16, "bfloat16")
    _sb("KT%d" % _d, 16, "float32")
for _n, _c, _t in (("wi", 1, "int32"), ("ki", 1, "int32"), ("sli", 256, "int32"), ("zin", 256, "bfloat16"),
                   ("IQ", 128, "int32"), ("IC", 128, "int32"), ("IC4", 128, "int32"), ("IQa", 128, "int32"), ("ip", 1, "int32"), ("ip4", 1, "int32"), ("ipm", 1, "int32"),
                   ("pg", 1, "float32"), ("kcol", 1, "float32"), ("TB", 1, "float32"), ("TD", 1, "float32"), ("ID", 128, "bfloat16"), ("IDh", 128, "float16"),
                   ("mI", 128, "bfloat16"), ("m64", 128, "bfloat16"), ("LI", 128, "bfloat16"), ("L2", 128, "bfloat16"),
                   ("PAR", 128, "bfloat16"), ("BLK", 128, "bfloat16"), ("GE", 128, "bfloat16"), ("TRI", 128, "bfloat16"),
                   ("SEL", 2048, "bfloat16"), ("EXP", 2048, "bfloat16"), ("ib", NB, "float32"), ("CI", NB, "bfloat16"),
                   ("CK", 3 * NB, "bfloat16"), ("NHC", 2 * NB, "bfloat16"), ("ROW", 256, "bfloat16"), ("sle", 256, "float32")):
    _sb(_n, _c, _t)
for _h in range(H):
    for _n, _c, _t in (("Oa", 16 * L + PAD, "bfloat16"), ("Ob", 16 * L + PAD, "bfloat16"), ("W", 6 * L, "bfloat16"), ("CM", 16 * L, "bfloat16"),
                       ("BM", 32 * L, "bfloat16"), ("OE", 2 * L, "bfloat16"), ("LT", 3 * L, "bfloat16"),
                       ("SF", L, "float32"), ("SU", L, "uint16"), ("OF", 2 * NB, "uint16"), ("NH", 2 * NB, "bfloat16"),
                       ("KK", 3 * NB, "float32"), ("FX", NB, "float32"), ("FE", NB, "float32"), ("FB", NB, "bfloat16"), ("DK", 2 * NB, "float32"),
                       ("ui", 2 * NB, "int32"), ("u", 2 * NB, "int32"), ("ub", 2 * NB, "float32"), ("u2", 2 * NB, "float16"),
                       ("sq", 2 * NB, "int32"), ("Fi", 2 * NB, "int32"), ("F2", 2 * NB, "float16"),
                       ("Xi", 32 * NB, "int32"), ("Xj", 32 * NB, "int32"), ("HL", 32 * NB, "uint16"), ("GB", max(1, SM_B) * 2 * L, "bfloat16"), ("MET", 2 * L, "bfloat16"),
                       ("NG", 2 * NB, "bfloat16"), ("r1", NB, "float32"), ("d1", NB, "float32"), ("n64", NB, "float32"), ("TH", NB, "float32"), ("r2", NB, "float32"),
                       ("BO", NB, "uint16"), ("BS", 2 * L, "bfloat16"), ("li", NB, "int32"), ("lj", NB, "int32"), ("lf", NB, "int32"), ("NL", NB, "uint16"),
                       ("PL", 2 * NB, "bfloat16"), ("MD", 2 * NB, "bfloat16"), ("NM_", L, "float32"), ("x1", L, "float32"),
                       ("IN", L, "bfloat16"), ("AC", 2 * L, "bfloat16"), ("VB", L, "bfloat16"),
                       ("vi", NB, "int32"), ("vu", NB, "int32"), ("vq", NB, "int32"), ("vF", NB, "int32"), ("vk", NB, "int32"), ("vs", NB, "int32"), ("vh", NB, "int32"), ("ZL", NB, "uint16"),
                       ("DF", L, "bfloat16"), ("zo", L, "bfloat16"), ("yf", L, "float32")):
        if H > 0:
            _sb("%s_%d" % (_n, _h), _c, _t)
_sb("BITO", 2 * VIS * NB * H, "bfloat16")
_sb("BITI", 2 * VIS * NB * H, "bfloat16")
for _s in ("sl", "x0", "wt", "kp", "z0", "cl"):
    SEMAPHORES.append("i" + _s)
for _d in range(1, 4):
    SEMAPHORES += ["aC%d" % _d, "aW%d" % _d]
for _t in range(VIS - 1):
    for _h in range(H):
        SEMAPHORES.append("bit%d_%d" % (_t, _h))
PACK = {}
_size = {}
for _n in list(SCRATCH):
    if _n[-2:] in ["_%d" % _h for _h in range(H)]:
        _w, _s, _t = SCRATCH.pop(_n)
        _k = "k%s_%s" % ({"float32": "f", "bfloat16": "b", "int32": "i", "uint16": "q", "float16": "h"}[_t], _n[-1])
        _o = _size.get((_k, _t), 0)
        PACK[_n] = (_k, _o)
        _size[(_k, _t)] = _o + (_s[1] + 31) // 32 * 32
for (_k, _t), _c in _size.items():
    _sb(_k, _c, _t)


def build(T, topo, core, Q):
    ops = []
    tagc = [""]
    hist = {}
    psg = {}
    ngrp = [0]

    def op(e, cost, fn, r=(), w=(), pr=(), pw=(), sig=None, after=(), first=None):
        i = len(ops)
        deps = {}

        def add(j, kind):
            if j != i:
                deps[j] = max(deps.get(j, 0), kind)
        for acc, wr in ((r, 0), (w, 1)):
            for b, lo, hi in acc:
                for (l2, h2, j, w2) in hist.setdefault(b, []):
                    if l2 < hi and lo < h2 and (wr or w2):
                        add(j, 2 if w2 else 1)
        for b, lo, hi in w:
            hist[b] = [x for x in hist[b] if not (lo <= x[0] and x[1] <= hi)] + [(lo, hi, i, 1)]
        for b, lo, hi in r:
            hist[b].append((lo, hi, i, 0))
        gids = []
        for acc, wr in ((pr, 0), (pw, 1)):
            for gid, lo, hi in acc:
                gr = psg.setdefault(gid, {"last": {}, "acc": [], "n": []})
                for e2, j in gr["last"].items():
                    if e2 != e:
                        add(j, 2)
                    elif e == "T":
                        add(j, 1)
                if e != "T":
                    for (l2, h2, j, w2) in gr["acc"]:
                        if l2 < hi and lo < h2 and (wr or w2) and ops[j]["e"] == e:
                            add(j, 2 if w2 else 1)
                gids.append((gid, lo, hi, wr))
        for gid, lo, hi, wr in gids:
            psg[gid]["last"][e] = i
            psg[gid]["acc"].append((lo, hi, i, wr))
            if i not in psg[gid]["n"]:
                psg[gid]["n"].append(i)
        for j in after:
            add(j, 0)
        ops.append({"e": e, "cost": cost, "fn": fn, "deps": deps, "g": sorted({x[0] for x in gids}), "sig": sig, "tag": tagc[0]})
        return i

    def grp():
        ngrp[0] += 1
        return ngrp[0]

    def S(name, lo, hi, step=1):
        b, o = PACK.get(name, (name, 0))
        t = T[b]
        return (t[:, o + lo:o + hi] if step == 1 else t[:, o + lo:o + hi:step]), (b, o + lo, o + hi)

    def PSl(gid, lo, hi, step=1):
        return ("ps", gid, lo, hi, step), (gid, lo, hi)

    def run(e, cost, call, out, ins, idx=None, extra_r=()):
        r, w, pr, pw = list(extra_r), [], [], []
        for x in ins:
            (pr if isinstance(x[0], tuple) else r).append(x[1])
        (pw if isinstance(out[0], tuple) else w).append(out[1])

        def ap(x, P):
            if isinstance(x[0], tuple):
                _, gid, lo, hi, st = x[0]
                return P(gid)[:, lo:hi] if st == 1 else P(gid)[:, lo:hi:st]
            return x[0]
        return op(e, cost, lambda P: call(ap(out, P), *[ap(x, P) for x in ins]), r, w, pr, pw)

    V, SC, TE, G, SY = Q["V"], Q["S"], Q["T"], Q["G"], Q["Y"]
    vc = lambda n: 30 + max(64, n) * VCY
    gc = lambda n: 60 + n * GCY * VCY
    tt = lambda out, a, b, o, n: run("V", vc(n), lambda x, y, z: V.tensor_tensor(x, y, z, o), out, [a, b])
    ts = lambda out, a, s1, s2, o0, o1, n: run("V", vc(n), (lambda x, y: V.tensor_scalar(x, y, s1, s2, o0, o1)) if o1 is not None else (lambda x, y: V.tensor_scalar(x, y, s1, s2, o0)), out, [a])
    cp = lambda out, a, n: run("V", vc(n), lambda x, y: V.tensor_copy(x, y), out, [a])

    def tsc(out, a, col, o, n, s2=None, o1=None):
        return run("V", vc(n), (lambda x, y, c: V.tensor_scalar(x, y, c, s2, o, o1)) if o1 is not None else (lambda x, y, c: V.tensor_scalar(x, y, c, None, o)), out, [a, col])

    def act(out, a, f, n, bias=0.0, scale=1.0):
        return run("S", vc(n), lambda x, y: SC.activation(x, y, f, bias=bias, scale=scale), out, [a])

    def actb(out, a, f, n, col):
        return run("S", vc(n), lambda x, y, c: SC.activation(x, y, f, bias=c), out, [a, col])

    def actsc(out, a, n, col):
        return run("S", vc(n), lambda x, y, c: SC.activation(x, y, F.Identity, scale=c), out, [a, col])

    def mm(lst):
        r, pw, cost = [], [], 40.0
        for o, a, b, s0, s1 in lst:
            r += [a[1], b[1]]
            pw.append(o[1])
            _, gid, lo, hi, st = o[0]
            cost += max(64, (hi - lo + st - 1) // st) * TC

        def fn(P):
            for o, a, b, s0, s1 in lst:
                _, gid, lo, hi, st = o[0]
                x = TE.matmul(P(gid)[:, lo:hi] if st == 1 else P(gid)[:, lo:hi:st], a[0], b[0], s0, s1)
            return x
        r = sorted(set(r))
        return op("T", cost, fn, r, (), (), sorted(set(pw)))

    def gat(e, out, win, off, n):
        if e == "V":
            return run("V", gc(n), lambda x, y, z: V.tensor_copy(x, y.indirect(z)), out, [win, off])
        return run("S", gc(n) + 15, lambda x, y, z: SC.activation(x, y.indirect(z), F.Copy), out, [win, off])

    def gtt(out, win, off, in1, o, n):
        return run("V", gc(n), lambda x, y, z, b: V.tensor_tensor(x, y.indirect(z), b, o), out, [win, off, in1])

    def fill(out, c, n):
        return run("V", vc(n), lambda x: V.memset(x, c), out, [])

    rank = T.rank_of(core)
    def load(dst, src, sem, cost):
        op("Y", 80, lambda P: SY.dma_start(dst[0], src), (), [dst[1]], sig=(sem, 16, cost))
    load(S("sli", 0, 256), T.sl[:], "isl", 2500)
    load(S("X", 0, 4096), T.x0[:], "ix0", 6000)
    load(S("wi", 0, 1), T.wt[:], "iwt", 6200)
    load(S("ki", 0, 1), T.kp[:], "ikp", 6300)
    load(S("zin", 0, 256), T.z0[:], "iz0", 6500)
    load(S("C0", 0, 4096), T.cl[:], "icl", 9000)
    it = lambda out, pat, base, cm, n: run("G", 150 + 2 * n * VCY, lambda x: G.iota(x, pat, base, cm, allow_small_or_imprecise_dtypes=True), out, [])
    it(S("IQ", 0, 128), [[1, 128]], 128, -1, 128)
    it(S("IC", 0, 128), [[1, 128]], 0, 0, 128)
    it(S("ip", 0, 1), [[0, 1]], 0, 1, 1)
    it(S("ib", 0, NB), [[16, NB]], 0, 0, NB)
    it(S("ROW", 0, 256), [[16, 256]], 0, 0, 256)

    def send(src, dname, sem, to, n, cost):
        rid, pid, _e = topo.addr(to)
        m = topo.mask(core, to)
        k = len(topo.engines(core, to))
        return op("G", 300, lambda P: G.remote_dma(T[dname][:, n[0]:n[1]], src[0], T.sem[sem], T.sem.ls, pid, rid, m), [src[1]], (), sig=("ls", k, None))

    fill(S("X", 4096, 4096 + PAD), 0.0, 16)
    ts(S("sle", 0, 256), S("sli", 0, 256), 0, 4097, A.is_lt, A.mult, 256)
    for h in range(H):
        tt(S("SF_%d" % h, 0, L), S("sli", h * L, (h + 1) * L), S("sle", h * L, (h + 1) * L), A.add, 2 * L)
        cp(S("SU_%d" % h, 0, L), S("SF_%d" % h, 0, L), L)

    def gather_O(t, h):
        tagc[0] = "O%d%d" % (t, h)
        o = "%s_%d" % ("Oa" if t % 2 == 0 else "Ob", h)
        q = L // NP
        for j in range(NP):
            gat("V" if j < GV else "S", S(o, 16 * q * j, 16 * q * (j + 1)), S("X", 0, 4096 + PAD), S("SU_%d" % h, q * j, q * (j + 1)), 16 * q)
    for h in range(H):
        for o in ("Oa", "Ob"):
            fill(S("%s_%d" % (o, h), 16 * L, 16 * L + PAD), 0.0, 16)
    tagc[0] = "const"
    b128 = lambda n: S(n, 0, 128)
    ts(b128("ID"), b128("IQ"), 128, None, A.is_equal, None, 128)
    ts(b128("mI"), b128("ID"), -1, None, A.mult, None, 64)
    for h in range(H):
        gather_O(0, h)
    ts(S("ip4", 0, 1), S("ip", 0, 1), 4, None, A.arith_shift_right, None, 1)
    cp(S("pg", 0, 1), S("ip4", 0, 1), 1)
    ts(b128("IC4"), b128("IC"), 4, None, A.arith_shift_right, None, 128)
    tsc(b128("BLK"), b128("IC4"), S("pg", 0, 1), A.is_equal, 128)
    fill(S("SEL", 0, 2048), 0.0, 1024)
    for a in range(16):
        cp(S("SEL", a * 128 + a, a * 128 + 128, 16), S("BLK", 0, 128, 16), 8)
    ts(b128("GE"), b128("IQ"), 128, None, A.is_ge, None, 128)
    tt(b128("TRI"), b128("BLK"), b128("GE"), A.mult, 256)
    ts(S("ipm", 0, 1), S("ip", 0, 1), 15, None, A.bitwise_and, None, 1)
    cp(S("kcol", 0, 1), S("ipm", 0, 1), 1)
    tsc(S("CI", 0, NB), S("ib", 0, NB), S("kcol", 0, 1), A.add, NB)
    fill(S("CK", 2 * NB, 3 * NB), 0.0, NB)
    for j in range(2):
        ts(S("CK", j * NB, (j + 1) * NB), S("CI", 0, NB), 16, None, A.mult, None, NB)
        ts(S("NHC", j * NB, (j + 1) * NB), S("CI", 0, NB), 16, 16, A.mult, A.add, NB)
    for h in range(H):
        cp(S("W_%d" % h, 0, L), S("zin", h * L, h * L + L), L // 2)
        cp(S("W_%d" % h, L, 2 * L), S("zin", h * L, h * L + L), L // 2)
    cp(S("WK0", 0, 1), S("wi", 0, 1), 1)
    cp(S("WK0", 1, 2), S("ki", 0, 1), 1)
    ext = {}
    sends = []
    for d in (1, 2, 3):
        to = T.cores[(rank - d) % N]
        sends.append(send(S("WK0", 0, 2), "WK%d" % d, "aW%d" % d, to, (0, 2), 0))
    for d in (1, 2, 3):
        to = T.cores[(rank - d) % N]
        sends.append(send(S("C0", 0, 4096), "C%d" % d, "aC%d" % d, to, (0, 4096), 0))
    nin = len(topo.engines(T.cores[(rank + 1) % N], core))
    for d in (1, 2, 3):
        op("X", 0, None, (), [S("WK%d" % d, 0, 2)[1]], sig=("aW%d" % d, nin, 2500), after=[sends[d - 1]])
        op("X", 0, None, (), [S("C%d" % d, 0, 4096)[1]], sig=("aC%d" % d, nin, 2000 + 6000 * d), after=[sends[d + 2]])
    ts(b128("IDh"), b128("IQ"), 128, None, A.is_equal, None, 128)
    ts(b128("IQa"), b128("IQ"), 15, None, A.bitwise_and, None, 128)
    ts(b128("PAR"), b128("IQa"), 0, None, A.is_equal, None, 128)

    def judge_tables(d):
        tagc[0] = "J%d" % d
        wk = "WK%d" % d
        if d == 1:
            tsc(S("WA%d" % d, 0, 2048), S("SEL", 0, 2048), S(wk, 0, 1), A.mult, 1024)
        else:
            actsc(S("WA%d" % d, 0, 2048), S("SEL", 0, 2048), 2048, S(wk, 0, 1))
        tsc(S("KR%d" % d, 0, 16), S("PAR", 0, 16), S(wk, 1, 2), A.mult, 16)
        g1 = grp()
        mm([(PSl(g1, 0, 16), b128("BLK"), S("KR%d" % d, 0, 16), True, True)])
        cp(S("KT%d" % d, 0, 16), PSl(g1, 0, 16), 16)
        if d:
            for m in range(16):
                tsc(S("KD%d" % d, m * 128, m * 128 + 128), b128("IDh"), S("KT%d" % d, m, m + 1), A.mult, 64)
    judge_tables(1)
    for n, c in (("m64", -64), ("LI", L), ("L2", 2 * L)):
        ts(b128(n), b128("ID"), c, None, A.mult, None, 64)
    ts(S("TB", 0, 1), S("kcol", 0, 1), SM_B - 0.5, -7.5, A.is_gt, A.mult, 1)
    ts(S("TB", 0, 1), S("TB", 0, 1), -1.0, None, A.add, None, 1)
    ts(S("TD", 0, 1), S("kcol", 0, 1), SK_D - 0.5, 4.0, A.is_gt, A.mult, 1)
    ts(S("TD", 0, 1), S("TD", 0, 1), 7.5, None, A.add, None, 1)
    for a in range(16):
        tsc(S("EXP", a * 128, a * 128 + 128), b128("BLK"), S("PAR", a, a + 1), A.mult, 64)
    judge_tables(0)

    SELs = lambda a: S("SEL", a * 128, a * 128 + 128)
    C2 = 25165824.0

    def comp(out, lo, hi, mat, name, s, e, stop=True):
        return [(out, S(mat, a * 128, a * 128 + 128), S(name, s + a, e, 16), a == 0, stop and a == 15) for a in range(16)]

    def mix(s):
        return sorted(range(16), key=lambda m: (m / s if m < s else (m - s) / (16 - s)))

    def stage_A(t, h):
        tagc[0] = "A%d%d" % (t, h)
        n = lambda x: "%s_%d" % (x, h)
        O = n("Oa" if t % 2 == 0 else "Ob")
        kper = 512 // L
        for k0 in range(0, SK_A, kper):
            gd = grp()
            lst = []
            for k in range(k0, k0 + kper):
                o = PSl(gd, (k - k0) * L, (k - k0 + 1) * L)
                lst.append((o, b128("ID"), S(O, k, 16 * L, 16), True, False))
                lst.append((o, b128("mI"), S(n("W"), 0, L), False, True))
            mm(lst)
            act(S(n("CM"), k0 * L, (k0 + kper) * L), PSl(gd, 0, kper * L), F.Relu, kper * L)
        if SK_A < 16:
            gz = grp()
            mm([(PSl(gz, 0, L), b128("ID"), S(n("W"), 0, L), True, True)])
            for k in range(SK_A, 16):
                tt(S(n("CM"), k * L, (k + 1) * L), S(O, k, 16 * L, 16), PSl(gz, 0, L), A.is_gt, L)
        gk = grp()
        for j, k in enumerate(mix(SK_A)):
            mm([(PSl(gk, 0, L), SELs(k), S(n("CM"), k * L, (k + 1) * L), j == 0, j == 15)])
        act(S(n("OE"), L, 2 * L), S(n("SF"), 0, L), F.Relu, L, bias=-4095.0)
        act(S(n("OE"), 0, L), PSl(gk, 0, L), F.Sign, L)
        gp = grp()
        mm([(PSl(gp, 0, 2 * L), b128("TRI"), S(n("OE"), 0, 2 * L), True, True)])
        act(S(n("LT"), L, 3 * L), PSl(gp, 0, 2 * L), F.Relu, 2 * L, bias=1.0, scale=-1.0)
        ts(S(n("LT"), 0, L), PSl(gp, 0, L), 2, None, A.is_lt, None, L)
        gq = grp()
        o = PSl(gq, 0, 3 * NB)
        mm(comp(o, 0, 0, "SEL", n("LT"), 0, 3 * L, False) + [(o, b128("ID"), S("CK", 0, 3 * NB), False, True)])
        cp(S(n("OF"), 0, 2 * NB), PSl(gq, 0, 2 * NB), 2 * NB)
        gtt(S(n("W"), 2 * L, 4 * L), S(O, 0, 16 * L + PAD), S(n("OF"), 0, 2 * NB), S(n("W"), 0, 2 * L), A.min, 2 * L)
        act(S(n("W"), 4 * L, 6 * L), S(n("W"), 2 * L, 4 * L), F.Copy, 2 * L)
        tt(S(n("NH"), 0, 2 * NB), PSl(gq, 0, 2 * NB), S("NHC", 0, 2 * NB), A.is_equal, 2 * NB)
        tt(S(n("KK"), 0, 3 * NB), PSl(gq, 0, 3 * NB), S("CK", 0, 3 * NB), A.subtract, 3 * NB)
        ts(S(n("FX"), 0, NB), S(n("KK"), 2 * NB, 3 * NB), 16, t - 16, A.is_ge, A.mult, NB)
        tt(S(n("FE"), 0, NB), S(n("KK"), 2 * NB, 3 * NB), S(n("FX"), 0, NB), A.add, NB)
        for j in range(2):
            tt(S(n("DK"), j * NB, (j + 1) * NB), S(n("KK"), j * NB, (j + 1) * NB), S(n("FE"), 0, NB), A.subtract, NB)
        cp(S(n("FB"), 0, NB), S(n("FE"), 0, NB), NB)

    def stage_B(t, h):
        tagc[0] = "B%d%d" % (t, h)
        n = lambda x: "%s_%d" % (x, h)
        d = 1 + t % 3
        W2 = 2 * NB
        g1 = grp()
        mm(comp(PSl(g1, 0, W2), 0, 0, "WA%d" % d, n("W"), 2 * L, 4 * L))
        q = lambda x: S(n(x), 0, W2)
        cp(q("ui"), PSl(g1, 0, W2), W2)
        ts(q("u"), q("ui"), 4095, None, A.bitwise_and, None, W2)
        tt(q("sq"), q("u"), q("u"), A.mult, W2)
        ts(q("ub"), q("u"), 2048, -4096, A.is_ge, A.mult, W2)
        ts(q("Fi"), q("sq"), 5, 4095, A.arith_shift_right, A.bitwise_and, W2)
        tt(q("u2"), q("u"), q("ub"), A.add, W2)
        ts(q("F2"), q("Fi"), -2048, None, A.add, None, W2)
        gx = grp()
        lst = []
        for m in range(16):
            o = PSl(gx, m * W2, (m + 1) * W2)
            lst.append((o, S("KD%d" % d, m * 128, m * 128 + 128), q("u2"), True, False))
            lst.append((o, b128("IDh"), q("F2"), False, True))
        mm(lst)
        x = lambda b: S(n(b), 0, 16 * W2)
        ts(x("Xi"), PSl(gx, 0, 16 * W2), 2048 + 97 * t, None, A.add, None, 16 * W2)
        ts(x("Xj"), x("Xi"), 4095, None, A.bitwise_and, None, 16 * W2)
        cp(x("HL"), x("Xj"), 16 * W2)
        for m in range(SM_B):
            gat("S", S(n("GB"), m * 2 * L, (m + 1) * 2 * L), S("C%d" % d, 0, 4096), S(n("HL"), m * W2, (m + 1) * W2), 2 * L)
            gd = grp()
            o = PSl(gd, 0, 2 * L)
            mm([(o, b128("ID"), S(n("W"), 2 * L, 4 * L), True, False), (o, b128("mI"), S(n("GB"), m * 2 * L, (m + 1) * 2 * L), False, True)])
            actb(S(n("BM"), m * 2 * L, (m + 1) * 2 * L), o, F.Sign, 2 * L, S("half", 0, 1))
        m = SM_B
        while m < 16:
            c = min(2, 16 - m)
            gtt(S(n("BM"), m * 2 * L, (m + c) * 2 * L), S("C%d" % d, 0, 4096), S(n("HL"), m * W2, (m + c) * W2), S(n("W"), 2 * L, (2 + 2 * c) * L), A.is_le, 2 * L * c)
            m += c
        gk = grp()
        for j, m in enumerate(mix(SM_B)):
            mm([(PSl(gk, 0, 2 * L), SELs(m), S(n("BM"), m * 2 * L, (m + 1) * 2 * L), j == 0, j == 15)])
        actb(S(n("MET"), 0, 2 * L), PSl(gk, 0, 2 * L), F.Sign, 2 * L, S("TB", 0, 1))
        gn = grp()
        lst = comp(PSl(gn, 0, W2), 0, 0, "SEL", n("MET"), 0, 2 * L, False)
        if t:
            b0 = ((t - 1) * H + h) * 2 * NB
            lst.append((PSl(gn, NB, W2), b128("mI"), S("BITI", b0, b0 + NB), False, False))
        lst.append((PSl(gn, 0, W2), b128("m64"), S(n("NH"), 0, W2), False, True))
        mm(lst)
        th = 2 * (AT[t] - 8)
        N1, N2 = S(n("NG"), NB, W2), S(n("NG"), 0, NB)
        c = lambda x: S(n(x), 0, NB)
        ts(N1, PSl(gn, NB, W2), th, None, A.is_ge, None, NB)
        gs = grp()
        mm([(PSl(gs, 0, NB), b128("PAR"), N1, True, True)])
        ts(c("n64"), N1, 64, th, A.mult, A.add, NB)
        ts(c("r1"), PSl(gs, 0, NB), C2, C2, A.add, A.subtract, NB)
        tt(c("d1"), PSl(gs, 0, NB), c("r1"), A.not_equal, NB)
        tt(c("TH"), c("d1"), c("n64"), A.add, NB)
        tt(N2, PSl(gn, 0, NB), c("TH"), A.is_ge, NB)
        gb = grp()
        o = PSl(gb, 0, NB)
        mm([(o, b128("ID"), S("CI", 0, NB), True, False), (o, b128("L2"), N1, False, False), (o, b128("LI"), N2, False, True)])
        cp(c("BO"), o, NB)
        gat("V", S(n("BS"), 0, L), S(n("W"), L, 4 * L), c("BO"), L)
        if t < VIS - 1:
            g2 = grp()
            mm([(PSl(g2, 0, NB), b128("PAR"), N2, True, True)])
            ts(c("r2"), PSl(g2, 0, NB), C2, C2, A.add, A.subtract, NB)
            b0 = (t * H + h) * 2 * NB
            tt(S("BITO", b0, b0 + NB), PSl(g2, 0, NB), c("r2"), A.not_equal, NB)
            q_ = (rank + 1 + t % 3) % N
            p2 = (q_ - 1 - (t + 1) % 3) % N
            sn = "bit%d_%d" % (t, h)
            j = send(S("BITO", b0, b0 + NB), "BITI", sn, T.cores[p2], (b0, b0 + NB), 0)
            src = [r for r in range(N) if ((r + 1 + t % 3) - 1 - (t + 1) % 3) % N == rank][0]
            op("X", 0, None, (), [S("BITI", b0, b0 + NB)[1]], sig=(sn, len(topo.engines(T.cores[src], core)), 2500), after=[j])

    def stage_C(t, h):
        tagc[0] = "C%d%d" % (t, h)
        n = lambda x: "%s_%d" % (x, h)
        c = lambda x: S(n(x), 0, NB)
        g1 = grp()
        mm(comp(PSl(g1, 0, NB), 0, 0, "WA0", n("BS"), 0, L))
        cp(c("li"), PSl(g1, 0, NB), NB)
        ts(c("lj"), c("li"), 15, None, A.bitwise_and, None, NB)
        tt(c("lf"), c("lj"), S("CK", 0, NB), A.add, NB)
        cp(c("NL"), c("lf"), NB)
        x = S("X", h * 16 * L, (h + 1) * 16 * L)
        run("V", 60 + L * 3 * VCY, lambda o, i, f: V.tensor_copy(o.indirect(f), i), x, [S(n("BS"), 0, L), c("NL")])
        cp(S(n("PL"), 0, NB), c("lj"), NB)
        tt(S(n("MD"), 0, 2 * NB), S(n("DK"), 0, 2 * NB), S(n("NG"), 0, 2 * NB), A.mult, 2 * NB)
        gp = grp()
        o = PSl(gp, 0, NB)
        mm([(o, b128("ID"), c("FB"), True, False), (o, b128("ID"), S(n("MD"), 0, NB), False, False), (o, b128("ID"), S(n("MD"), NB, 2 * NB), False, True)])
        act(S(n("PL"), NB, 2 * NB), o, F.Copy, NB)
        ge = grp()
        lst = [(PSl(ge, a, 2 * L, 16), S("EXP", a * 128, a * 128 + 128), S(n("PL"), 0, 2 * NB), True, True) for a in range(16)]
        mm(lst)
        lo, pu = PSl(ge, 0, L), PSl(ge, L, 2 * L)
        nm = S(n("NM_"), 0, L)
        tsc(nm, pu, S("kcol", 0, 1), A.not_equal, L, 16384.0, A.mult)
        act(pu, nm, F.Identity, L, bias=16384.0, scale=-1.0)
        tt(S(n("x1"), 0, L), S(n("SF"), 0, L), pu, A.max, L)
        tt(nm, nm, S("ROW", h * L, (h + 1) * L), A.add, 2 * L)
        tt(lo, lo, nm, A.add, L)
        tt(S(n("SF"), 0, L), S(n("x1"), 0, L), lo, A.min, L)
        if t < VIS - 1:
            cp(S(n("SU"), 0, L), S(n("SF"), 0, L), L)

    def stage_D(t, h):
        tagc[0] = "D%d%d" % (t, h)
        n = lambda x: "%s_%d" % (x, h)
        O = n("Oa" if t % 2 == 0 else "Ob")
        gb = grp()
        mm([(PSl(gb, 0, L), b128("ID"), S(n("BS"), 0, L), True, True)])
        kper = 512 // L
        for k0 in range(0, SK_D, kper):
            gd = grp()
            lst = []
            for k in range(k0, min(SK_D, k0 + kper)):
                o = PSl(gd, (k - k0) * L, (k - k0 + 1) * L)
                lst += [(o, b128("mI"), S(O, k, 16 * L, 16), True, False), (o, b128("ID"), S(n("BS"), 0, L), False, True)]
            mm(lst)
            w = (min(SK_D, k0 + kper) - k0) * L
            actb(S(n("CM"), k0 * L, k0 * L + w), PSl(gd, 0, w), F.Sign, w, S("half", 0, 1))
        for k in range(SK_D, 16):
            tt(S(n("CM"), k * L, (k + 1) * L), S(O, k, 16 * L, 16), PSl(gb, 0, L), A.is_le, L)
        gk = grp()
        for j, k in enumerate(mix(SK_D)):
            mm([(PSl(gk, 0, L), SELs(k), S(n("CM"), k * L, (k + 1) * L), j == 0, j == 15)])
        tsc(S(n("IN"), 0, L), PSl(gk, 0, L), S("TD", 0, 1), A.is_lt, L, -512.0, A.mult)
        act(S(n("BS"), L, 2 * L), S(n("BS"), 0, L), F.Copy, L)
        prev = S(n("BS"), 0, 2 * L)
        kper = 512 // L
        for k0 in range(0, 16, kper):
            ge = grp()
            lst = []
            for k in range(k0, k0 + kper):
                o = PSl(ge, (k - k0) * L, (k - k0 + 1) * L)
                lst += [(o, b128("ID"), S(O, k, 16 * L, 16), True, False), (o, S("EXP", k * 128, k * 128 + 128), S(n("IN"), 0, L), False, True)]
            mm(lst)
            for j in range(0, 512, 2 * L):
                tt(S(n("AC"), 0, 2 * L), prev, PSl(ge, j, j + 2 * L), A.max, 2 * L)
                prev = S(n("AC"), 0, 2 * L)
        vb = S(n("VB"), 0, L)
        tt(vb, S(n("AC"), 0, L), S(n("AC"), L, 2 * L), A.max, 2 * L)
        c = lambda x: S(n(x), 0, NB)
        g1 = grp()
        mm(comp(PSl(g1, 0, NB), 0, 0, "WA0", n("VB"), 0, L))
        cp(c("vi"), PSl(g1, 0, NB), NB)
        ts(c("vu"), c("vi"), 4095, None, A.bitwise_and, None, NB)
        tt(c("vq"), c("vu"), c("vu"), A.mult, NB)
        tsc(c("vk"), c("vu"), S("KT0", 0, 1), A.mult, NB, 97.0 * t, A.add)
        ts(c("vF"), c("vq"), 5, None, A.arith_shift_right, None, NB)
        tt(c("vs"), c("vF"), c("vk"), A.add, NB)
        ts(c("vh"), c("vs"), 4095, None, A.bitwise_and, None, NB)
        cp(c("ZL"), c("vh"), NB)
        gtt(S(n("DF"), 0, L), S("C0", 0, 4096), c("ZL"), vb, A.subtract, L)
        if t < VIS - 1:
            act(S(n("W"), 0, L), S(n("DF"), 0, L), F.Abs, L)
            act(S(n("W"), L, 2 * L), S(n("DF"), 0, L), F.Abs, L)
        else:
            act(S(n("zo"), 0, L), S(n("DF"), 0, L), F.Abs, L)
            z = S(n("zo"), 0, L)
            op("Y", 80, lambda P: SY.dma_start(T.yz[:, h * L:(h + 1) * L], z[0]), [z[1]], (), sig=("out", 16, None))

    def outs(h):
        n = lambda x: "%s_%d" % (x, h)
        x = S("X", h * 16 * L, (h + 1) * 16 * L)
        op("Y", 80, lambda P: SY.dma_start(T.yx[:, h * 16 * L:(h + 1) * 16 * L], x[0]), [x[1]], (), sig=("out", 16, None))
        ts(S(n("x1"), 0, L), S(n("SF"), 0, L), 4096, -4097, A.is_ge, A.mult, L)
        y = S(n("yf"), 0, L)
        tt(y, S(n("SF"), 0, L), S(n("x1"), 0, L), A.add, 2 * L)
        op("Y", 80, lambda P: SY.dma_start(T.yl[:, h * L:(h + 1) * L], y[0]), [y[1]], (), sig=("out", 16, None))

    fill(S("half", 0, 1), 0.5, 1)
    for t in range(VIS):
        for h in range(H):
            stage_A(t, h)
        if t in (0, 1):
            judge_tables(t + 2)
        for h in range(H):
            stage_B(t, h)
        for h in range(H):
            stage_C(t, h)
        if t < VIS - 1:
            for h in range(H):
                gather_O(t + 1, h)
        else:
            for h in range(H):
                outs(h)
        for h in range(H):
            stage_D(t, h)
    return ops, psg


_sb("half", 1, "float32")


def schedule(ops, psg):
    n = len(ops)
    succ = [[] for _ in range(n)]
    left = [0] * n
    for i, o in enumerate(ops):
        for j in o["deps"]:
            succ[j].append(i)
            left[i] += 1
    prio = [0.0] * n
    for i in range(n - 1, -1, -1):
        o = ops[i]
        dur = o["cost"] + (o["sig"][2] or 2000 if o["sig"] else 0)
        prio[i] = dur + max([prio[j] + LAT for j in succ[i]] or [0])
    for i in range(n):
        tg = ops[i]["tag"]
        prio[i] += BON.get(tg[:1] + tg[2:], 0.0)
    free = {e: 0.0 for e in "VSTGYX"}
    fin = [0.0] * n
    start = [0.0] * n
    ready = [0.0] * n
    avail = {e: [] for e in free}
    for i in range(n):
        if left[i] == 0:
            avail[ops[i]["e"]].append(i)
    bank_of, bank_free, bank_dep = {}, {b: 0.0 for b in range(8)}, {b: [] for b in range(8)}
    remain = {g: len(x["n"]) for g, x in psg.items()}
    order = []
    for _ in range(n):
        best = None
        for e, lst in avail.items():
            cand = None
            nb = min(bank_free.values()) if bank_free else None
            for i in lst:
                r = ready[i]
                new = [g for g in ops[i]["g"] if g not in bank_of]
                if new:
                    if not bank_free:
                        continue
                    r = max(r, nb)
                s = max(r, free[e]) if e != "X" else r
                key = (s, -prio[i])
                if cand is None or key < cand[0]:
                    cand = (key, i)
            if cand and (best is None or cand[0] < best[0]):
                best = cand
        if best is None:
            raise ValueError("no bank")
        (s, _p), i = best
        o = ops[i]
        e = o["e"]
        avail[e].remove(i)
        for g in o["g"]:
            if g not in bank_of:
                b = min(bank_free, key=lambda k: bank_free[k])
                bank_of[g] = b
                bank_free.pop(b)
                for j in bank_dep[b]:
                    o["deps"].setdefault(j, 1 if ops[j]["e"] == e else 2)
        start[i] = s
        f = s + o["cost"]
        free[e] = f
        fin[i] = f + (o["sig"][2] or 0 if o["sig"] else 0)
        order.append(i)
        for g in o["g"]:
            remain[g] -= 1
            if remain[g] == 0:
                b = bank_of[g]
                bank_free[b] = max(fin[j] for j in psg[g]["n"]) + LAT
                last = {}
                for j in psg[g]["n"]:
                    last[ops[j]["e"]] = j if ops[j]["e"] not in last or start[j] > start[last[ops[j]["e"]]] else last[ops[j]["e"]]
                bank_dep[b] = list(last.values())
        for j in succ[i]:
            left[j] -= 1
            kind = ops[j]["deps"][i]
            ready[j] = max(ready[j], fin[i] + LAT if not (ops[j]["e"] == e and kind == 1) else start[i])
            if left[j] == 0:
                avail[ops[j]["e"]].append(j)
    return order, bank_of, start, fin


def rank_program(g, core, T, topo):
    if T.rank_of(core) is None:
        return
    Q = {"V": g.vector, "S": g.scalar, "T": g.tensor, "G": g, "Y": g.sync}
    ops, psg = build(T, topo, core, Q)
    order, bank_of, start, fin = schedule(ops, psg)
    P = lambda gid: T["p%d" % bank_of[gid]]
    count = {e: 0 for e in "VSTG"}
    know = {e: {} for e in "VSTGY"}
    done = {e: {} for e in "VSTG"}
    sigv, sigc = {}, {}
    total = {}

    def merge(a, b):
        for k, v in b.items():
            if a.get(k, 0) < v:
                a[k] = v
    for i in order:
        o = ops[i]
        e = o["e"]
        if e != "X":
            need = {}
            for j, kind in o["deps"].items():
                if kind == 0 or (kind == 1 and ops[j]["e"] == e and ops[j]["sig"] is None):
                    continue
                if kind == 1 and ops[j]["e"] == e:
                    continue
                s, v = sigv[j]
                if s == "ls" or s == "out":
                    continue
                if need.get(s, (0, 0))[0] < v:
                    need[s] = (v, j)
            for s in sorted(need, key=lambda s: -start[need[s][1]]):
                v, j = need[s]
                if know[e].get(s, 0) < v:
                    Q[e].wait_ge(T.sem[s], v)
                    merge(know[e], sigc[j])
            ins = o["fn"](P)
        if o["sig"] is None:
            count[e] += 1
            s = "e" + e
            ins.then_inc(T.sem[s], 1)
            sigv[i] = (s, count[e])
            merge(done[e], know[e])
            done[e][s] = count[e]
            sigc[i] = dict(done[e])
            total[s] = count[e]
        else:
            s, v, _c = o["sig"]
            if e == "Y":
                ins.then_inc(T.sem[s], v)
            total[s] = total.get(s, 0) + v
            sigv[i] = (s, v)
            sigc[i] = dict(know[e]) if e != "X" else {}
            sigc[i][s] = v
    for s in sorted(total):
        if know["G"].get(s, 0) < total[s]:
            g.wait_ge(T.sem[s], total[s])
